import numpy as np
import ml_dtypes


def mxq(x, axis, fmt="e4m3"):
    dtype, down = {"e4m3": (ml_dtypes.float8_e4m3fn, 7), "e5m2": (ml_dtypes.float8_e5m2, 14)}[fmt]
    v = np.moveaxis(np.asarray(x, np.float32).astype(ml_dtypes.bfloat16).astype(np.float64), axis, -1)
    blocks = v.reshape(v.shape[:-1] + (-1, 32))
    amax = np.abs(blocks).max(-1, keepdims=True)
    byte = np.maximum(np.where(amax > 0, np.frexp(amax)[1] - 1 + 127, 0) - down, 1)
    scale = np.exp2(byte - 127.0)
    codes = (blocks / scale).astype(np.float32).astype(dtype).astype(np.float64)
    return np.moveaxis((codes * scale).reshape(v.shape), -1, axis)


WIDE = False


def mx_kscale(k):
    if not WIDE:
        return np.ones(k)
    levels = np.array([10, -10, 5, -5, 0])
    if k % 512:
        return np.exp2(np.random.permutation(np.resize(levels, k // 32))).repeat(32)
    a = np.empty((k // 512, 16))
    for p in range(k // 512):
        a[p, :8] = np.random.permutation(np.resize(levels, 8))
        for g in range(8):
            far = levels[np.abs(levels - a[p, g]) >= 10]
            a[p, g + 8] = far[np.random.randint(len(far))]
    return np.exp2(a.ravel()).repeat(32)


def f64(x):
    return np.asarray(x).astype(np.float64)


def striped(idx):
    return np.tile(idx.reshape(-1, 16).T, (8, 1)).astype(np.uint16)


def unstriped(offs):
    return offs[:16].T.reshape(-1).astype(np.int64)


def striped8(idx):
    return np.concatenate([x.reshape(-1, 16).T for x in idx]).astype(np.uint16)


def runs(offs, k):
    lists = np.stack([offs[16 * r : 16 * r + 16].T.reshape(-1) for r in range(8)]).astype(np.int64)
    return lists[np.arange(k) % 512 // 64]


def pack_weight(w):
    k, n = w.shape
    w = f64(np.asarray(w, np.float32).astype(ml_dtypes.bfloat16)).reshape(k // 32, 32, n)
    amax = np.abs(w).max(1)
    byte = np.clip(np.where(amax > 0, np.frexp(amax)[1] - 1 + 127 - 7, 1), 1, 254)
    scaled = (w * np.exp2(127.0 - byte)[:, None, :]).reshape(k, n).astype(np.float32)
    words = np.ascontiguousarray(scaled.reshape(k // 512, 128, 4, n).transpose(0, 1, 3, 2)).astype(ml_dtypes.float8_e4m3fn).view(np.uint8)
    return words, np.ascontiguousarray(byte.astype(np.uint8).reshape(k // 512, 16, n))


def unpack_weight(words, scales):
    g, p, n, _ = words.shape
    vals = np.ascontiguousarray(words).view(ml_dtypes.float8_e4m3fn).astype(np.float64) * np.repeat(np.exp2(scales.astype(np.float64) - 127.0), 8, axis=1)[..., None]
    return vals.transpose(0, 1, 3, 2).reshape(g * 512, n)


K, T, S, N, G, H = 512, 1024, 256, 512, 2048, 512


def setup_inputs():
    n = np.random.standard_normal
    s = mx_kscale(K)[:, None]
    u = mx_kscale(K)
    packed_xT = pack_weight(n((K, T)) * s)
    packed_dT = pack_weight(n((K, G)) / s)
    return {
        "x_words": packed_xT[0],
        "x_scales": packed_xT[1],
        "d_words": packed_dT[0],
        "d_scales": packed_dT[1],
        "gn": (np.random.uniform(0.5, 1.5, (H, 1)) * u[:, None]).astype(np.float32),
        "w1": (n((H, N)) / np.sqrt(2 * H) / u[:, None]).astype(np.float32),
        "w2": (n((K, N)) / np.sqrt(2 * K) / s).astype(np.float32),
        "offs": striped(np.random.permutation(T)[:S]),
        "k1": striped8(np.random.randint(0, G, (8, H))),
        "n1": striped8(np.stack([np.random.permutation(S) for _ in range(8)])),
        "n2": striped8(np.stack([np.random.permutation(S) for _ in range(8)])),
        "n3": striped8(np.stack([np.random.permutation(S) for _ in range(8)])),
        "two": striped(np.random.permutation(T)[:S]),
        "n4": striped(np.random.permutation(S)),
        "n5": striped(np.random.permutation(S)),
        "n6": striped(np.random.permutation(S)),
    }


def reference(x_words, x_scales, d_words, d_scales, gn, w1, w2, offs, k1, n1, n2, n3, two, n4, n5, n6):
    d_k1 = unpack_weight(d_words, d_scales)[np.arange(K)[:, None], runs(k1, K)]
    xq = unpack_weight(x_words, x_scales)[:, unstriped(offs)]
    h = 0.0625 * (d_k1.T @ xq)
    st = h - (h[np.arange(H)[:, None], runs(n1, H)])
    su = np.maximum(st, st[np.arange(H)[:, None], runs(n2, H)])
    z = f64(gn) * (su + 0.5 * (su[np.arange(H)[:, None], runs(n3, H)]))
    x_two = unpack_weight(x_words, x_scales)[:, unstriped(two)]
    h2 = mxq(f64(w1), 0, "e4m3").T @ mxq(z, 0, "e4m3") + mxq(f64(w2), 0, "e4m3").T @ x_two
    return h2 + h2[:, unstriped(n4)] - (np.maximum(h2[:, unstriped(n5)], h2[:, unstriped(n6)]))

@@ -1,0 +1,231 @@
+from contextlib import ExitStack
+
+import concourse.mybir as mybir
+
+K, T, S, N, G, H = 512, 1024, 256, 512, 2048, 512
+FLOPS = 2 * K * H * S + 2 * H * N * S + 2 * K * N * S
+
+F32 = mybir.dt.float32
+BF16 = mybir.dt.bfloat16
+I32 = mybir.dt.int32
+U32 = mybir.dt.uint32
+U16 = mybir.dt.uint16
+U8 = mybir.dt.uint8
+X4 = mybir.dt.float8_e4m3fn_x4
+ALU = mybir.AluOpType
+COPY = mybir.ActivationFunctionType.Copy
+
+P = 128
+PACK = 4
+WIDE = 2 * S
+NARROW = S + 16
+HALF = S // 2
+
+
+def tile_picked_pqmixthreetrim_none_p_kernel(
+    tc, x_words, x_scales, d_words, d_scales, gn, w1, w2, offs, k1, n1, n2, n3, two, n4, n5, n6, out
+):
+    nc = tc.nc
+    with ExitStack() as ctx:
+        lists = ctx.enter_context(tc.tile_pool(name="lists", bufs=1))
+        keep = ctx.enter_context(tc.tile_pool(name="keep", bufs=1))
+        psum = ctx.enter_context(tc.psum_pool(name="psum", bufs=1))
+
+        def sb(shape, dtype, name, tag=None):
+            return keep.tile(shape, dtype, name=name, tag=tag or name, align_bytes=64)
+
+        def load_list(src, name):
+            tile = lists.tile([P, src.shape[1]], U16, name=name)
+            nc.sync.dma_start(tile[:], src)
+            return tile
+
+        def load_words(src, name):
+            tile = sb([P, src.shape[2]], I32, name)
+            nc.sync.dma_start(tile[:], src[0].rearrange("p n t -> p (n t)").bitcast(I32))
+            return tile
+
+        def load_weight(src, name):
+            tile = sb([P, PACK, N], F32, name)
+            nc.sync.dma_start(tile[:], src.rearrange("(p j) n -> p j n", j=PACK))
+            return tile
+
+        x_scale_win = sb([P, T], U8, "x_scale_win")
+        nc.vector.memset(x_scale_win[:].bitcast(I32), 0)
+        for q in range(4):
+            nc.scalar.dma_start(
+                x_scale_win[32 * q : 32 * q + 4, :].bitcast(I32), x_scales[0, 4 * q : 4 * q + 4, :].bitcast(I32)
+            )
+        k1_l = load_list(k1, "k1_l")
+        d_scale_win = sb([P, G], U8, "d_scale_win")
+        nc.sync.dma_start(
+            d_scale_win[:].bitcast(I32), d_scales[0].bitcast(I32).unsqueeze(1).to_broadcast([16, 8, G // 4])
+        )
+        offs_l = load_list(offs, "offs_l")
+        d_word_win = load_words(d_words, "d_word_win")
+        x_word_win = load_words(x_words, "x_word_win")
+        n1_l = load_list(n1, "n1_l")
+        two_l = load_list(two, "two_l")
+        w2_raw = load_weight(w2, "w2_raw")
+        n2_l = load_list(n2, "n2_l")
+        w1_raw = load_weight(w1, "w1_raw")
+        n3_l = load_list(n3, "n3_l")
+        n5_l = load_list(n5, "n5_l")
+        n6_l = load_list(n6, "n6_l")
+        n4_l = load_list(n4, "n4_l")
+        gain = sb([P, PACK], F32, "gain")
+        nc.gpsimd.dma_start(gain[:], gn.rearrange("(p t) o -> p (t o)", t=PACK))
+
+        d_scale = sb([P, H], U8, "d_scale")
+        nc.vector.memset(d_scale[:].bitcast(I32), 0)
+        h_win = [sb([P, WIDE], F32, "h_win%d" % t) for t in range(PACK)]
+        h2_win = [sb([P, NARROW], F32, "h2_win%d" % t) for t in range(PACK)]
+        for t in range(PACK):
+            nc.vector.memset(h_win[t][:, S:], 0.0)
+        for t in range(PACK):
+            nc.vector.memset(h2_win[t][:, S:], 0.0)
+
+        d_scale_got = sb([P, H], U8, "d_scale_got")
+        nc.vector.tensor_copy(d_scale_got[:], d_scale_win[:].indirect(k1_l[:]))
+        d_scale_dealt = sb([P, H], U8, "d_scale_dealt")
+        nc.vector.tensor_copy(
+            d_scale_dealt[:].rearrange("p (t m) -> p t m", t=PACK),
+            d_scale_got[:].rearrange("p (m t) -> p t m", t=PACK),
+        )
+        for q in range(4):
+            nc.scalar.dma_start(
+                d_scale[32 * q : 32 * q + 4, :].bitcast(I32), d_scale_dealt[32 * q : 32 * q + 32 : 8, :].bitcast(I32)
+            )
+
+        def pick_words(offsets, name, tag=None):
+            words = sb([P, S], U32, name, tag)
+            nc.vector.tensor_copy(words[:], x_word_win[:].bitcast(U32).indirect(offsets[:]))
+            return words
+
+        def pick_scales(offsets, name, tag=None):
+            scales = sb([P, S], U8, name, tag)
+            nc.vector.tensor_copy(scales[:], x_scale_win[:].indirect(offsets[:]))
+            return scales
+
+        xq_scales = pick_scales(offs_l, "xq_scales")
+        d_word_got = sb([P, H], U32, "d_word_got")
+        nc.vector.tensor_copy(d_word_got[:], d_word_win[:].bitcast(U32).indirect(k1_l[:]))
+        d_word = sb([P, H], I32, "d_word")
+        nc.vector.tensor_copy(
+            d_word[:].rearrange("p (t c i) -> p c t i", t=PACK, i=4),
+            d_word_got[:].bitcast(I32).rearrange("p (c i t) -> p c t i", t=PACK, i=4),
+        )
+        xq_words = pick_words(offs_l, "xq_words")
+
+        def block(t):
+            return slice(t * P, (t + 1) * P)
+
+        h_ps = [psum.tile([P, S], F32, name="h_ps%d" % t) for t in range(PACK)]
+        for t in range(PACK):
+            nc.tensor.matmul_mx(
+                h_ps[t][:], lhsT=d_word[:, block(t)].bitcast(X4), lhsT_scale=d_scale[:, block(t)],
+                rhs=xq_words[:].bitcast(X4), rhs_scale=xq_scales[:], start=True, stop=True,
+            )
+
+        def scalar_copy(dst, src):
+            nc.scalar.activation(dst, src, COPY)
+
+        def weave(planes, name, tag, copy=nc.vector.tensor_copy):
+            woven = sb([P, P * PACK], BF16, name + "_woven", tag)
+            copy(
+                woven[:].rearrange("p (c i j) -> p c j i", j=PACK, i=4),
+                planes.rearrange("p j (c i) -> p c j i", i=4),
+            )
+            return woven
+
+        def quantise(woven, name):
+            words = sb([P, P], U32, name + "_words")
+            scales = sb([P, P], U8, name + "_scales")
+            nc.vector.quantize_mx(words[:].bitcast(X4), scales[:], woven[:])
+            return words, scales
+
+        def fetch(dst, window, offsets):
+            nc.scalar.activation(dst, window[:].indirect(offsets), COPY)
+
+        st_win = [sb([P, WIDE], F32, "st_win%d" % t) for t in range(PACK)]
+        su_win = [sb([P, WIDE], F32, "su_win%d" % t) for t in range(PACK)]
+        su_gain = sb([P, PACK, S], F32, "su_gain")
+        half_gain = sb([P, PACK], F32, "half_gain")
+        su_n3 = sb([P, PACK, S], F32, "su_n3")
+        z = sb([P, PACK, S], F32, "z")
+        h2_ps = [psum.tile([P, S], F32, name="h2_ps%d" % t) for t in range(PACK)]
+        w1_q, w2_q, z_q = {}, {}, {}
+
+        nc.vector.tensor_scalar(half_gain[:], gain[:], 0.5, None, ALU.mult)
+        for t in range(PACK):
+            nc.vector.tensor_scalar(h_win[t][:, :S], h_ps[t][:], 0.0625, None, ALU.mult)
+        for t in range(PACK):
+            fetch(st_win[t][:, S:], h_win[t], n1_l[:])
+            nc.vector.tensor_tensor(st_win[t][:, :S], h_win[t][:, :S], st_win[t][:, S:], ALU.subtract)
+        x2_words = pick_words(two_l, "x2_words", "h_win0")
+        x2_scales = pick_scales(two_l, "x2_scales", "h_win2")
+
+        for t in range(PACK):
+            fetch(su_win[t][:, S:], st_win[t], n2_l[:])
+            nc.vector.tensor_tensor(su_win[t][:, :S], st_win[t][:, :S], su_win[t][:, S:], ALU.max)
+            nc.vector.tensor_scalar(su_gain[:, t, :], su_win[t][:, :S], gain[:, t : t + 1], None, ALU.mult)
+        w2_q[0] = quantise(weave(w2_raw[:, :, block(0)], "w2_0", "h_win3"), "w2_0")
+        w1_q[0] = quantise(weave(w1_raw[:, :, block(0)], "w1_0", "st_win1"), "w1_0")
+
+        for u in range(2):
+            cols = slice(u * HALF, (u + 1) * HALF)
+            for t in range(PACK):
+                fetch(su_n3[:, t, cols], su_win[t], n3_l[:, u * HALF // 16 : (u + 1) * HALF // 16])
+                nc.vector.scalar_tensor_tensor(
+                    z[:, t, cols], su_n3[:, t, cols], half_gain[:, t : t + 1], su_gain[:, t, cols], ALU.mult, ALU.add
+                )
+            z_q[u] = quantise(weave(z[:, :, cols], "z%d" % u, "woven%d" % u), "z%d" % u)
+
+        def second(t, copy):
+            nc.tensor.matmul_mx(
+                h2_ps[t][:], lhsT=w2_q[t][0][:].bitcast(X4), lhsT_scale=w2_q[t][1][:],
+                rhs=x2_words[:].bitcast(X4), rhs_scale=x2_scales[:], start=True, stop=False,
+            )
+            for u in range(2):
+                nc.tensor.matmul_mx(
+                    h2_ps[t][:, u * HALF : (u + 1) * HALF], lhsT=w1_q[t][0][:].bitcast(X4), lhsT_scale=w1_q[t][1][:],
+                    rhs=z_q[u][0][:].bitcast(X4), rhs_scale=z_q[u][1][:], start=False, stop=(u == 1),
+                )
+            copy(h2_win[t][:, :S], h2_ps[t][:])
+
+        got = sb([P, PACK, 3, S], F32, "got")
+        top = sb([P, PACK, S], F32, "top")
+        rest = sb([P, PACK, S], F32, "rest")
+        res = sb([P, PACK, S], F32, "res")
+
+        def finish(t):
+            nc.vector.tensor_tensor(top[:, t, :], got[:, t, 0, :], got[:, t, 1, :], ALU.max)
+            nc.vector.tensor_tensor(rest[:, t, :], h2_win[t][:, :S], top[:, t, :], ALU.subtract)
+            nc.vector.tensor_tensor(res[:, t, :], rest[:, t, :], got[:, t, 2, :], ALU.add)
+            nc.sync.dma_start(out[block(t), :], res[:, t, :])
+
+        def fetch_three(t):
+            fetch(got[:, t, 0, :], h2_win[t], n5_l[:])
+            fetch(got[:, t, 1, :], h2_win[t], n6_l[:])
+            fetch(got[:, t, 2, :], h2_win[t], n4_l[:])
+
+        def weights(t):
+            w2_q[t] = quantise(weave(w2_raw[:, :, block(t)], "w2_%d" % t, "woven1"), "w2_%d" % t)
+            w1_q[t] = quantise(weave(w1_raw[:, :, block(t)], "w1_%d" % t, "woven1"), "w1_%d" % t)
+
+        w2_woven = weave(w2_raw[:, :, block(1)], "w2_1", "su_win2", scalar_copy)
+        w1_woven = weave(w1_raw[:, :, block(1)], "w1_1", "su_win3", scalar_copy)
+        second(0, scalar_copy)
+        fetch_three(0)
+        w2_q[1] = quantise(w2_woven, "w2_1")
+        w1_q[1] = quantise(w1_woven, "w1_1")
+        second(1, nc.vector.tensor_copy)
+        fetch_three(1)
+        weights(2)
+        second(2, nc.vector.tensor_copy)
+        fetch_three(2)
+        finish(0)
+        weights(3)
+        second(3, nc.vector.tensor_copy)
+        fetch_three(3)
+        for t in range(1, PACK):
+            finish(t)

@@ -44,36 +44,36 @@ def tile_picked_pqmixthreetrim_none_p_kernel(
             nc.sync.dma_start(tile[:], src[0].rearrange("p n t -> p (n t)").bitcast(I32))
             return tile
 
-        def load_weight(src, name):
-            tile = sb([P, PACK, N], F32, name)
+        def load_weight(src, name, tag=None):
+            tile = sb([P, PACK, N], F32, name, tag)
             nc.sync.dma_start(tile[:], src.rearrange("(p j) n -> p j n", j=PACK))
             return tile
 
+        d_scale_win = sb([P, G], U8, "d_scale_win")
+        nc.vector.memset(d_scale_win[:, : G // 2].bitcast(I32), 0)
+        nc.gpsimd.memset(d_scale_win[:, G // 2 :].bitcast(I32), 0)
         x_scale_win = sb([P, T], U8, "x_scale_win")
-        nc.vector.memset(x_scale_win[:].bitcast(I32), 0)
         for q in range(4):
             nc.scalar.dma_start(
-                x_scale_win[32 * q : 32 * q + 4, :].bitcast(I32), x_scales[0, 4 * q : 4 * q + 4, :].bitcast(I32)
+                x_scale_win[32 * q : 32 * q + 32, :].bitcast(I32),
+                x_scales[0, 4 * q : 4 * q + 4, :].bitcast(I32).unsqueeze(0).to_broadcast([8, 4, T // 4]),
             )
         k1_l = load_list(k1, "k1_l")
-        d_scale_win = sb([P, G], U8, "d_scale_win")
-        nc.sync.dma_start(
-            d_scale_win[:].bitcast(I32), d_scales[0].bitcast(I32).unsqueeze(1).to_broadcast([16, 8, G // 4])
-        )
+        nc.sync.dma_start(d_scale_win[0:P:8, :].bitcast(I32), d_scales[0].bitcast(I32))
         offs_l = load_list(offs, "offs_l")
         d_word_win = load_words(d_words, "d_word_win")
         x_word_win = load_words(x_words, "x_word_win")
-        n1_l = load_list(n1, "n1_l")
         two_l = load_list(two, "two_l")
-        w2_raw = load_weight(w2, "w2_raw")
+        n1_l = load_list(n1, "n1_l")
         n2_l = load_list(n2, "n2_l")
+        gain = sb([P, PACK], F32, "gain")
+        nc.sync.dma_start(gain[:], gn.rearrange("(p t) o -> p (t o)", t=PACK))
+        w2_raw = load_weight(w2, "w2_raw")
         w1_raw = load_weight(w1, "w1_raw")
         n3_l = load_list(n3, "n3_l")
         n5_l = load_list(n5, "n5_l")
         n6_l = load_list(n6, "n6_l")
         n4_l = load_list(n4, "n4_l")
-        gain = sb([P, PACK], F32, "gain")
-        nc.gpsimd.dma_start(gain[:], gn.rearrange("(p t) o -> p (t o)", t=PACK))
 
         d_scale = sb([P, H], U8, "d_scale")
         nc.vector.memset(d_scale[:].bitcast(I32), 0)
@@ -143,26 +143,25 @@ def tile_picked_pqmixthreetrim_none_p_kernel(
             nc.vector.quantize_mx(words[:].bitcast(X4), scales[:], woven[:])
             return words, scales
 
-        def fetch(dst, window, offsets):
-            nc.scalar.activation(dst, window[:].indirect(offsets), COPY)
+        def fetch(dst, window, offsets, scale=1.0):
+            nc.scalar.activation(dst, window[:].indirect(offsets), COPY, scale=scale)
 
         st_win = [sb([P, WIDE], F32, "st_win%d" % t) for t in range(PACK)]
         su_win = [sb([P, WIDE], F32, "su_win%d" % t) for t in range(PACK)]
         su_gain = sb([P, PACK, S], F32, "su_gain")
-        half_gain = sb([P, PACK], F32, "half_gain")
         su_n3 = sb([P, PACK, S], F32, "su_n3")
         z = sb([P, PACK, S], F32, "z")
         h2_ps = [psum.tile([P, S], F32, name="h2_ps%d" % t) for t in range(PACK)]
         w1_q, w2_q, z_q = {}, {}, {}
 
-        nc.vector.tensor_scalar(half_gain[:], gain[:], 0.5, None, ALU.mult)
-        for t in range(PACK):
+        nc.scalar.activation(h_win[0][:, :S], h_ps[0][:], COPY, scale=0.0625)
+        for t in range(1, PACK):
             nc.vector.tensor_scalar(h_win[t][:, :S], h_ps[t][:], 0.0625, None, ALU.mult)
         for t in range(PACK):
             fetch(st_win[t][:, S:], h_win[t], n1_l[:])
             nc.vector.tensor_tensor(st_win[t][:, :S], h_win[t][:, :S], st_win[t][:, S:], ALU.subtract)
-        x2_words = pick_words(two_l, "x2_words", "h_win0")
-        x2_scales = pick_scales(two_l, "x2_scales", "h_win2")
+        x2_words = pick_words(two_l, "x2_words")
+        x2_scales = pick_scales(two_l, "x2_scales", "h_win0")
 
         for t in range(PACK):
             fetch(su_win[t][:, S:], st_win[t], n2_l[:])
@@ -174,9 +173,9 @@ def tile_picked_pqmixthreetrim_none_p_kernel(
         for u in range(2):
             cols = slice(u * HALF, (u + 1) * HALF)
             for t in range(PACK):
-                fetch(su_n3[:, t, cols], su_win[t], n3_l[:, u * HALF // 16 : (u + 1) * HALF // 16])
+                fetch(su_n3[:, t, cols], su_win[t], n3_l[:, u * HALF // 16 : (u + 1) * HALF // 16], 0.5)
                 nc.vector.scalar_tensor_tensor(
-                    z[:, t, cols], su_n3[:, t, cols], half_gain[:, t : t + 1], su_gain[:, t, cols], ALU.mult, ALU.add
+                    z[:, t, cols], su_n3[:, t, cols], gain[:, t : t + 1], su_gain[:, t, cols], ALU.mult, ALU.add
                 )
             z_q[u] = quantise(weave(z[:, :, cols], "z%d" % u, "woven%d" % u), "z%d" % u)
 
@@ -192,40 +191,58 @@ def tile_picked_pqmixthreetrim_none_p_kernel(
                 )
             copy(h2_win[t][:, :S], h2_ps[t][:])
 
-        got = sb([P, PACK, 3, S], F32, "got")
-        top = sb([P, PACK, S], F32, "top")
+        at_n5 = sb([P, PACK, S], F32, "at_n5")
+        at_n6 = sb([P, PACK, S], F32, "at_n6")
         rest = sb([P, PACK, S], F32, "rest")
         res = sb([P, PACK, S], F32, "res")
+        at_n4 = {}
+
+        def fetch_pair(t):
+            fetch(at_n5[:, t, :], h2_win[t], n5_l[:])
+            fetch(at_n6[:, t, :], h2_win[t], n6_l[:])
+
+        def fetch_n4(t, tag=None):
+            at_n4[t] = sb([P, S], F32, "at_n4_%d" % t, tag)
+            fetch(at_n4[t][:], h2_win[t], n4_l[:])
+
+        def less_larger(t):
+            larger = sb([P, S], F32, "larger%d" % t)
+            nc.vector.tensor_tensor(larger[:], at_n5[:, t, :], at_n6[:, t, :], ALU.max)
+            nc.vector.tensor_tensor(rest[:, t, :], h2_win[t][:, :S], larger[:], ALU.subtract)
 
         def finish(t):
-            nc.vector.tensor_tensor(top[:, t, :], got[:, t, 0, :], got[:, t, 1, :], ALU.max)
-            nc.vector.tensor_tensor(rest[:, t, :], h2_win[t][:, :S], top[:, t, :], ALU.subtract)
-            nc.vector.tensor_tensor(res[:, t, :], rest[:, t, :], got[:, t, 2, :], ALU.add)
+            nc.vector.tensor_tensor(res[:, t, :], rest[:, t, :], at_n4[t][:], ALU.add)
             nc.sync.dma_start(out[block(t), :], res[:, t, :])
-
-        def fetch_three(t):
-            fetch(got[:, t, 0, :], h2_win[t], n5_l[:])
-            fetch(got[:, t, 1, :], h2_win[t], n6_l[:])
-            fetch(got[:, t, 2, :], h2_win[t], n4_l[:])
 
         def weights(t):
             w2_q[t] = quantise(weave(w2_raw[:, :, block(t)], "w2_%d" % t, "woven1"), "w2_%d" % t)
             w1_q[t] = quantise(weave(w1_raw[:, :, block(t)], "w1_%d" % t, "woven1"), "w1_%d" % t)
 
-        w2_woven = weave(w2_raw[:, :, block(1)], "w2_1", "su_win2", scalar_copy)
-        w1_woven = weave(w1_raw[:, :, block(1)], "w1_1", "su_win3", scalar_copy)
+        w2_woven1 = weave(w2_raw[:, :, block(1)], "w2_1", "su_win1", scalar_copy)
+        w1_woven1 = weave(w1_raw[:, :, block(1)], "w1_1", "su_win2", scalar_copy)
+        w2_woven2 = weave(w2_raw[:, :, block(2)], "w2_2", "su_win3", scalar_copy)
         second(0, scalar_copy)
-        fetch_three(0)
-        w2_q[1] = quantise(w2_woven, "w2_1")
-        w1_q[1] = quantise(w1_woven, "w1_1")
+        fetch_pair(0)
+        fetch_n4(0)
+        w2_q[1] = quantise(w2_woven1, "w2_1")
+        w1_q[1] = quantise(w1_woven1, "w1_1")
         second(1, nc.vector.tensor_copy)
-        fetch_three(1)
-        weights(2)
+        fetch_pair(1)
+        fetch_n4(1)
+        w2_q[2] = quantise(w2_woven2, "w2_2")
+        w1_q[2] = quantise(weave(w1_raw[:, :, block(2)], "w1_2", "woven1"), "w1_2")
         second(2, nc.vector.tensor_copy)
-        fetch_three(2)
+        fetch_pair(2)
+        less_larger(0)
         finish(0)
         weights(3)
         second(3, nc.vector.tensor_copy)
-        fetch_three(3)
-        for t in range(1, PACK):
-            finish(t)
+        fetch_pair(3)
+        less_larger(1)
+        fetch_n4(2, "larger1")
+        fetch_n4(3)
+        finish(1)
+        less_larger(2)
+        less_larger(3)
+        finish(2)
+        finish(3)

from contextlib import ExitStack

import concourse.mybir as mybir

K, T, S, N, G, H = 512, 1024, 256, 512, 2048, 512
FLOPS = 2 * K * H * S + 2 * H * N * S + 2 * K * N * S

F32 = mybir.dt.float32
BF16 = mybir.dt.bfloat16
I32 = mybir.dt.int32
U32 = mybir.dt.uint32
U16 = mybir.dt.uint16
U8 = mybir.dt.uint8
X4 = mybir.dt.float8_e4m3fn_x4
ALU = mybir.AluOpType
COPY = mybir.ActivationFunctionType.Copy

P = 128
PACK = 4
WIDE = 2 * S
NARROW = S + 16
HALF = S // 2


def tile_picked_pqmixthreetrim_none_p_kernel(
    tc, x_words, x_scales, d_words, d_scales, gn, w1, w2, offs, k1, n1, n2, n3, two, n4, n5, n6, out
):
    nc = tc.nc
    with ExitStack() as ctx:
        lists = ctx.enter_context(tc.tile_pool(name="lists", bufs=1))
        keep = ctx.enter_context(tc.tile_pool(name="keep", bufs=1))
        psum = ctx.enter_context(tc.psum_pool(name="psum", bufs=1))

        def sb(shape, dtype, name, tag=None):
            return keep.tile(shape, dtype, name=name, tag=tag or name, align_bytes=64)

        def load_list(src, name):
            tile = lists.tile([P, src.shape[1]], U16, name=name)
            nc.sync.dma_start(tile[:], src)
            return tile

        def load_words(src, name):
            tile = sb([P, src.shape[2]], I32, name)
            nc.sync.dma_start(tile[:], src[0].rearrange("p n t -> p (n t)").bitcast(I32))
            return tile

        def load_weight(src, name, tag=None):
            tile = sb([P, PACK, N], F32, name, tag)
            nc.sync.dma_start(tile[:], src.rearrange("(p j) n -> p j n", j=PACK))
            return tile

        d_scale_win = sb([P, G], U8, "d_scale_win")
        nc.vector.memset(d_scale_win[:, : G // 2].bitcast(I32), 0)
        nc.gpsimd.memset(d_scale_win[:, G // 2 :].bitcast(I32), 0)
        x_scale_win = sb([P, T], U8, "x_scale_win")
        for q in range(4):
            nc.scalar.dma_start(
                x_scale_win[32 * q : 32 * q + 32, :].bitcast(I32),
                x_scales[0, 4 * q : 4 * q + 4, :].bitcast(I32).unsqueeze(0).to_broadcast([8, 4, T // 4]),
            )
        k1_l = load_list(k1, "k1_l")
        nc.sync.dma_start(d_scale_win[0:P:8, :].bitcast(I32), d_scales[0].bitcast(I32))
        offs_l = load_list(offs, "offs_l")
        d_word_win = load_words(d_words, "d_word_win")
        x_word_win = load_words(x_words, "x_word_win")
        two_l = load_list(two, "two_l")
        n1_l = load_list(n1, "n1_l")
        n2_l = load_list(n2, "n2_l")
        gain = sb([P, PACK], F32, "gain")
        nc.sync.dma_start(gain[:], gn.rearrange("(p t) o -> p (t o)", t=PACK))
        w2_raw = load_weight(w2, "w2_raw")
        w1_raw = load_weight(w1, "w1_raw")
        n3_l = load_list(n3, "n3_l")
        n5_l = load_list(n5, "n5_l")
        n6_l = load_list(n6, "n6_l")
        n4_l = load_list(n4, "n4_l")

        d_scale = sb([P, H], U8, "d_scale")
        nc.vector.memset(d_scale[:].bitcast(I32), 0)
        h_win = [sb([P, WIDE], F32, "h_win%d" % t) for t in range(PACK)]
        h2_win = [sb([P, NARROW], F32, "h2_win%d" % t) for t in range(PACK)]
        for t in range(PACK):
            nc.vector.memset(h_win[t][:, S:], 0.0)
        for t in range(PACK):
            nc.vector.memset(h2_win[t][:, S:], 0.0)

        d_scale_got = sb([P, H], U8, "d_scale_got")
        nc.vector.tensor_copy(d_scale_got[:], d_scale_win[:].indirect(k1_l[:]))
        d_scale_dealt = sb([P, H], U8, "d_scale_dealt")
        nc.vector.tensor_copy(
            d_scale_dealt[:].rearrange("p (t m) -> p t m", t=PACK),
            d_scale_got[:].rearrange("p (m t) -> p t m", t=PACK),
        )
        for q in range(4):
            nc.scalar.dma_start(
                d_scale[32 * q : 32 * q + 4, :].bitcast(I32), d_scale_dealt[32 * q : 32 * q + 32 : 8, :].bitcast(I32)
            )

        def pick_words(offsets, name, tag=None):
            words = sb([P, S], U32, name, tag)
            nc.vector.tensor_copy(words[:], x_word_win[:].bitcast(U32).indirect(offsets[:]))
            return words

        def pick_scales(offsets, name, tag=None):
            scales = sb([P, S], U8, name, tag)
            nc.vector.tensor_copy(scales[:], x_scale_win[:].indirect(offsets[:]))
            return scales

        xq_scales = pick_scales(offs_l, "xq_scales")
        d_word_got = sb([P, H], U32, "d_word_got")
        nc.vector.tensor_copy(d_word_got[:], d_word_win[:].bitcast(U32).indirect(k1_l[:]))
        d_word = sb([P, H], I32, "d_word")
        nc.vector.tensor_copy(
            d_word[:].rearrange("p (t c i) -> p c t i", t=PACK, i=4),
            d_word_got[:].bitcast(I32).rearrange("p (c i t) -> p c t i", t=PACK, i=4),
        )
        xq_words = pick_words(offs_l, "xq_words")

        def block(t):
            return slice(t * P, (t + 1) * P)

        h_ps = [psum.tile([P, S], F32, name="h_ps%d" % t) for t in range(PACK)]
        for t in range(PACK):
            nc.tensor.matmul_mx(
                h_ps[t][:], lhsT=d_word[:, block(t)].bitcast(X4), lhsT_scale=d_scale[:, block(t)],
                rhs=xq_words[:].bitcast(X4), rhs_scale=xq_scales[:], start=True, stop=True,
            )

        def scalar_copy(dst, src):
            nc.scalar.activation(dst, src, COPY)

        def weave(planes, name, tag, copy=nc.vector.tensor_copy):
            woven = sb([P, P * PACK], BF16, name + "_woven", tag)
            copy(
                woven[:].rearrange("p (c i j) -> p c j i", j=PACK, i=4),
                planes.rearrange("p j (c i) -> p c j i", i=4),
            )
            return woven

        def quantise(woven, name):
            words = sb([P, P], U32, name + "_words")
            scales = sb([P, P], U8, name + "_scales")
            nc.vector.quantize_mx(words[:].bitcast(X4), scales[:], woven[:])
            return words, scales

        def fetch(dst, window, offsets, scale=1.0):
            nc.scalar.activation(dst, window[:].indirect(offsets), COPY, scale=scale)

        st_win = [sb([P, WIDE], F32, "st_win%d" % t) for t in range(PACK)]
        su_win = [sb([P, WIDE], F32, "su_win%d" % t) for t in range(PACK)]
        su_gain = sb([P, PACK, S], F32, "su_gain")
        su_n3 = sb([P, PACK, S], F32, "su_n3")
        z = sb([P, PACK, S], F32, "z")
        h2_ps = [psum.tile([P, S], F32, name="h2_ps%d" % t) for t in range(PACK)]
        w1_q, w2_q, z_q = {}, {}, {}

        nc.scalar.activation(h_win[0][:, :S], h_ps[0][:], COPY, scale=0.0625)
        for t in range(1, PACK):
            nc.vector.tensor_scalar(h_win[t][:, :S], h_ps[t][:], 0.0625, None, ALU.mult)
        for t in range(PACK):
            fetch(st_win[t][:, S:], h_win[t], n1_l[:])
            nc.vector.tensor_tensor(st_win[t][:, :S], h_win[t][:, :S], st_win[t][:, S:], ALU.subtract)
        x2_words = pick_words(two_l, "x2_words")
        x2_scales = pick_scales(two_l, "x2_scales", "h_win0")

        for t in range(PACK):
            fetch(su_win[t][:, S:], st_win[t], n2_l[:])
            nc.vector.tensor_tensor(su_win[t][:, :S], st_win[t][:, :S], su_win[t][:, S:], ALU.max)
            nc.vector.tensor_scalar(su_gain[:, t, :], su_win[t][:, :S], gain[:, t : t + 1], None, ALU.mult)
        w2_q[0] = quantise(weave(w2_raw[:, :, block(0)], "w2_0", "h_win3"), "w2_0")
        w1_q[0] = quantise(weave(w1_raw[:, :, block(0)], "w1_0", "st_win1"), "w1_0")

        for u in range(2):
            cols = slice(u * HALF, (u + 1) * HALF)
            for t in range(PACK):
                fetch(su_n3[:, t, cols], su_win[t], n3_l[:, u * HALF // 16 : (u + 1) * HALF // 16], 0.5)
                nc.vector.scalar_tensor_tensor(
                    z[:, t, cols], su_n3[:, t, cols], gain[:, t : t + 1], su_gain[:, t, cols], ALU.mult, ALU.add
                )
            z_q[u] = quantise(weave(z[:, :, cols], "z%d" % u, "woven%d" % u), "z%d" % u)

        def second(t, copy):
            nc.tensor.matmul_mx(
                h2_ps[t][:], lhsT=w2_q[t][0][:].bitcast(X4), lhsT_scale=w2_q[t][1][:],
                rhs=x2_words[:].bitcast(X4), rhs_scale=x2_scales[:], start=True, stop=False,
            )
            for u in range(2):
                nc.tensor.matmul_mx(
                    h2_ps[t][:, u * HALF : (u + 1) * HALF], lhsT=w1_q[t][0][:].bitcast(X4), lhsT_scale=w1_q[t][1][:],
                    rhs=z_q[u][0][:].bitcast(X4), rhs_scale=z_q[u][1][:], start=False, stop=(u == 1),
                )
            copy(h2_win[t][:, :S], h2_ps[t][:])

        at_n5 = sb([P, PACK, S], F32, "at_n5")
        at_n6 = sb([P, PACK, S], F32, "at_n6")
        rest = sb([P, PACK, S], F32, "rest")
        res = sb([P, PACK, S], F32, "res")
        at_n4 = {}

        def fetch_pair(t):
            fetch(at_n5[:, t, :], h2_win[t], n5_l[:])
            fetch(at_n6[:, t, :], h2_win[t], n6_l[:])

        def fetch_n4(t, tag=None):
            at_n4[t] = sb([P, S], F32, "at_n4_%d" % t, tag)
            fetch(at_n4[t][:], h2_win[t], n4_l[:])

        def less_larger(t):
            larger = sb([P, S], F32, "larger%d" % t)
            nc.vector.tensor_tensor(larger[:], at_n5[:, t, :], at_n6[:, t, :], ALU.max)
            nc.vector.tensor_tensor(rest[:, t, :], h2_win[t][:, :S], larger[:], ALU.subtract)

        def finish(t):
            nc.vector.tensor_tensor(res[:, t, :], rest[:, t, :], at_n4[t][:], ALU.add)
            nc.sync.dma_start(out[block(t), :], res[:, t, :])

        def weights(t):
            w2_q[t] = quantise(weave(w2_raw[:, :, block(t)], "w2_%d" % t, "woven1"), "w2_%d" % t)
            w1_q[t] = quantise(weave(w1_raw[:, :, block(t)], "w1_%d" % t, "woven1"), "w1_%d" % t)

        w2_woven1 = weave(w2_raw[:, :, block(1)], "w2_1", "su_win1", scalar_copy)
        w1_woven1 = weave(w1_raw[:, :, block(1)], "w1_1", "su_win2", scalar_copy)
        w2_woven2 = weave(w2_raw[:, :, block(2)], "w2_2", "su_win3", scalar_copy)
        second(0, scalar_copy)
        fetch_pair(0)
        fetch_n4(0)
        w2_q[1] = quantise(w2_woven1, "w2_1")
        w1_q[1] = quantise(w1_woven1, "w1_1")
        second(1, nc.vector.tensor_copy)
        fetch_pair(1)
        fetch_n4(1)
        w2_q[2] = quantise(w2_woven2, "w2_2")
        w1_q[2] = quantise(weave(w1_raw[:, :, block(2)], "w1_2", "woven1"), "w1_2")
        second(2, nc.vector.tensor_copy)
        fetch_pair(2)
        less_larger(0)
        finish(0)
        weights(3)
        second(3, nc.vector.tensor_copy)
        fetch_pair(3)
        less_larger(1)
        fetch_n4(2, "larger1")
        fetch_n4(3)
        finish(1)
        less_larger(2)
        less_larger(3)
        finish(2)
        finish(3)
